import numpy as np, ml_dtypes
CORES = [3,7,11,15,131,135,139,143]
N = 8
BF = ml_dtypes.bfloat16
def gentries(a):
    return np.ascontiguousarray(a.reshape(8, 16, -1).transpose(0, 2, 1)).reshape(8, -1)
def gtable(e):
    e = np.asarray(e); return np.ascontiguousarray(e.reshape(8, -1, 16).transpose(0, 2, 1)).reshape(128, -1).astype(np.int32)
W, K, RO, S, TH, AG = 1664, 256, 2, 5, 66, 9
L0 = 16 - RO
B = K // N
def hubbed(rng, hub, n, share):
    return np.where(rng.random((N, 8, n)) < share, np.take_along_axis(hub, rng.integers(0, 32, (N, 8, n)), 2), rng.integers(0, W, (N, 8, n)))
def parts(rng):
    x = np.where(rng.random((N, 8, 1, W)) < 0.875, rng.integers(0, 16, (N, 8, 16, W)), rng.integers(4, 12, (N, 8, 16, W)))
    hub = rng.integers(0, W, (N, 8, 32)); a = hubbed(rng, hub, L0 * W, 0.1).reshape(N, 8, L0, W)
    a = np.where(rng.random(a.shape) < rng.choice(np.array([0.05, 0.2, 0.45]), (N, 8, 1, 1)), -1, a)
    return x, a, hubbed(rng, hub, W, 0.25), rng.integers(0, W, (N, 8, K))
def pack(x, a, s, p):
    a = np.concatenate([a, np.full((N, 8, RO, W), -1)], axis=2)
    return {"x0": np.ascontiguousarray(x.reshape(N, 128, W)).astype(np.float32).astype(BF), "lk": np.ascontiguousarray(a.reshape(N, 128, W)).astype(np.int32),
            "nx": np.ascontiguousarray(s).astype(np.int32), "w0": np.stack([gtable(e) for e in p])}
def setup_inputs(rng):
    return pack(*parts(rng))
def setup_inputs_ties(rng):
    x, a, s, p = parts(rng); h = W // 2
    x[..., :h] = rng.integers(0, 16, (N, 8, 16, h))
    t = TH - 1 + rng.integers(0, 3, (N, 8, 1, h)); o = np.argsort(rng.random((N, 8, 16, h)), axis=2)
    x[..., h:2 * h] = x[..., :h] + np.where(x[..., :h] < 8, 1, -1) * ((t >> 4) + (o < (t & 15)))
    i = np.arange(L0)[None, None, :, None]; at = rng.integers(0, L0, (N, 8, 1, h)); bare = rng.random((N, 8, 1, h)) < 0.5
    a[..., :h] = np.where(i == at, h + np.arange(h), np.where((i > at) | bare, -1, a[..., :h]))
    return pack(x, a, s, rng.integers(0, h, (N, 8, K)))
def setup_inputs_votes(rng):
    x, a, s, p = parts(rng); h = K // 2
    for q in range(N):
        for g in range(8):
            if q < N - 1 and g % 4 == 3: continue
            c = rng.permutation(W)[:K * (S + 1)].reshape(K, S + 1); a[q, g] = -1
            s[q, g, c[:, :S]] = c[:, 1:]
            if q == N - 1:
                y = rng.integers(5, 8, (16, K, S)); e = np.where(np.arange(K) < h, 15, rng.integers(8, 11, (16, K)))
                s[q, g, c[:h, S]] = c[h + rng.permutation(h), 2]
                p[q, g] = c[:, 0]
            elif g % 2 == 1:
                n = K - 1 if g == 1 else int(rng.integers(h, K))
                y = rng.integers(0, 8, (16, K, S)); y[rng.permutation(16)[AG - 1:], n] += 8
                e = rng.integers(0, 16, (16, K)); e[:, 0] = 8
                s[q, g, c[:, S - 1]] = c[0, S]
                p[q, g] = c[:, 0]
            else:
                y = rng.integers(2, 14, (16, K, S)); y[:, h:] = np.where(rng.random((1, K - h, 1)) < 0.5, 2, 13)
                z = y[:, :, 0]
                for k in range(1, S): z = (z + y[:, :, k]) >> 1
                o = np.argsort(rng.random((16, K)), axis=0); n = AG - 1 + rng.integers(0, 3, (1, K))
                e = z + np.where(o < n, rng.integers(1, 3, (16, K)), -rng.integers(0, 2, (16, K)))
                s[q, g, c[h:, S - 1]] = np.where(rng.random(K - h) < 0.75, c[:K - h, S], c[h:, S])
                p[q, g] = c[rng.permutation(K), 0]
            x[q, g][:, c[:, :S].reshape(-1)] = y.reshape(16, K * S); x[q, g][:, c[:, S]] = e
    return pack(x, a, s, p)
def setup_inputs_alike(rng):
    x, a, s, p = parts(rng); few = np.array([0, W - 1, W // 2, 5])
    a[:, ::2] = np.where(a[:, ::2] < 0, -1, rng.choice(few, (N, 4, L0, W)))
    a[:, 1] = np.where(a[:, 1] < 0, -1, np.arange(W)); s[:, 1] = np.arange(W)
    s[:, 0] = W - 1; s[:, 4] = 0; s[:, 2] = rng.choice(few, (N, W))
    p[:, 3] = p[:, 3, :1]; p[:, 5] = rng.choice(few, (N, K)); p[:, 6] = np.where(rng.random((N, K)) < 0.5, 0, W - 1)
    return pack(x, a, s, p)
def setup_inputs_full(rng):
    x, a, s, p = parts(rng)
    x[:, ::2] = rng.integers(6, 10, (N, 4, 16, W)); x[:, 1::2] = 15 * rng.integers(0, 2, (N, 4, 16, W))
    a = np.where(a < 0, rng.integers(0, W, a.shape), a)
    return pack(x, a, s, p)
def setup_inputs_spread(rng):
    x, a, s, p = parts(rng)
    x = np.minimum((np.exp2(1 + 3 * rng.random((N, 8, 1, W))) * rng.random((N, 8, 16, W))).astype(np.int64), 15)
    a = np.where(a < 0, -1, (W * rng.random(a.shape) ** 3).astype(np.int64)); s = (W * rng.random(s.shape) ** 2).astype(np.int64)
    return pack(x, np.minimum(a, W - 1), np.minimum(s, W - 1), p)
def check_inputs(d):
    bad = []
    x = d["x0"].astype(np.float32)
    if not np.all((x >= 0) & (x <= 15) & (x == np.floor(x))): bad.append("x0 whole numbers from 0 to 15")
    for k, lo in (("lk", -1), ("nx", 0), ("w0", 0)):
        if np.min(d[k]) < lo or np.max(d[k]) > W - 1: bad.append("range of " + k)
    if np.any(d["lk"].reshape(-1, 8, 16, W)[:, :, L0:] != -1): bad.append("upper links of lk empty")
    return bad
def reference(x0, lk, nx, w0):
    M = W + RO * K
    X = np.zeros((N, 8, 16, M), np.int64); X[..., :W] = x0.astype(np.float32).astype(np.int64).reshape(N, 8, 16, W)
    ad = np.full((N, 8, 16, M), -1, np.int64); ad[..., :W] = lk.reshape(N, 8, 16, W)
    sc = np.zeros((N, 8, M), np.int64); sc[..., :W] = nx
    v = np.stack([gentries(e) for e in w0]).astype(np.int64)
    i = np.arange(16)[:, None]
    for t in range(RO):
        n = W + t * K; Z = np.zeros((N, 8, 16, K), np.int64)
        for r in range(N):
            for g in range(8):
                x, a, s, p = X[r, g], ad[r, g], sc[r, g], v[r, g]
                z = x[:, p]; l = np.full(K, 16)
                for k in range(S):
                    c = a[:, p]
                    dist = np.add.reduce(np.abs(x[:, np.maximum(c, 0)] - z[:, None, :]), axis=0)
                    b = np.max(np.where((c >= 0) & (dist < TH) & (i < l), i, -1), axis=0)
                    p = np.where(b >= 0, c[np.maximum(b, 0), np.arange(K)], s[p]); l = np.where(b >= 0, b, l)
                    y = x[:, p]; yes = np.add.reduce((y > z).astype(np.int64), axis=0) >= AG
                    z = (z + y) >> 1
                Z[r, g] = z; v[r, g] = p
                ends = np.zeros(M, bool); ends[p] = True
                no = np.zeros(M, bool); no[p[~yes]] = True
                x[::2] = np.where(ends & ~no, 15 - x[::2], x[::2])
                u, first = np.unique(p, return_index=True)
                a[L0 + t, u] = n + first; s[n:n + K] = s[p]
        for r in range(N):
            for q in range(N):
                X[q, :, :, n + r * B:n + (r + 1) * B] = np.roll(Z[r, :, :, q * B:(q + 1) * B], (q - r) % N, axis=0)
    return {"yx": X.reshape(N, 128, M).astype(np.float32).astype(BF), "yv": v.astype(np.float32)}

@@ -1,0 +1,532 @@
+import numpy as np
+from concourse.bass import DstId, RemoteDMATransfer
+from concourse.mybir import dt, AluOpType as Op, AxisListType, ActivationFunctionType as AF
+
+W, K, RO, S = 1664, 256, 2, 5
+GB = 256
+N0 = GB + 8
+XC = N0 + W + RO * K
+AC = N0 + W + K
+MAGIC = 12582912.0
+KZ = 4
+
+SCRATCH = {}
+
+
+def declare(where, dtype, names, shape):
+    for nm in names.split():
+        SCRATCH[nm] = (where, shape, dtype)
+
+
+declare("sbuf", "bfloat16", "X", [128, XC])
+declare("sbuf", "int32", "A", [128, AC])
+declare("sbuf", "int32", "w0s KI", [128, 16])
+declare("sbuf", "uint16", "VO OFX OFA", [128, 16])
+declare("sbuf", "bfloat16", "Y GT FY RB LE LO ZS0 ZS1 ZERO WR", [128, 256])
+declare("sbuf", "bfloat16", "junk", [128, 1024])
+declare("sbuf", "float32", "VAL YV AD cF", [128, 256])
+declare("sbuf", "float32", "ACV DV FF FR M16 M5 MN TR", [128, 16])
+declare("sbuf", "float32", "ACS", [128, 32])
+declare("sbuf", "float32", "KF", [128, 40])
+declare("sbuf", "bfloat16", "LAA LAB LBB IB IP IN ZM MK DC WC T2 Z0 Z1 NV0 NV1", [128, 128])
+declare("sbuf", "float16", "IH TRI PERM BLK WB WH AH0 AH1 LT0 LT1 HH0 HH1", [128, 128])
+declare("sbuf", "float32", "tF SAME PW", [128, 128])
+declare("sbuf", "int32", "cmI cgI", [128, 128])
+declare("sbuf", "int32", "cI", [128, 256])
+declare("sbuf", "int32", "pI", [128, 1])
+declare("sbuf", "bfloat16", "B2 BN B1 B4", [128, 8])
+declare("sbuf", "float16", "BH", [128, 8])
+declare("sbuf", "float16", "CT", [128, 256])
+declare("sbuf", "bfloat16", "D0 D1 M0 M1", [128, 2048])
+declare("sbuf", "uint16", "AO0 AO1", [128, 128])
+declare("sbuf", "bfloat16", "NT0 NT1", [128, 136])
+declare("sbuf", "float16", "SA0 SA1", [128, S * 128])
+declare("psum", "float32", "eA eB dist0 dist1 ch0 ch1 zp0 zp1", [128, 512])
+SEMAPHORES = ["qV", "qP", "qS", "qG", "ldw", "ldx", "ldal", "ldas", "ldn", "arr0", "arr1", "snt", "out1", "out2", "out3"]
+
+
+def rank_program(g, core, T, topo):
+    rank = T.rank_of(core)
+    if rank is None:
+        return
+    sem = T.sem
+    eng = {"V": g.vector, "P": g.tensor, "S": g.scalar, "G": g, "Y": g.sync}
+    qsem = {"V": "qV", "P": "qP", "S": "qS", "G": "qG"}
+    clock = {q: {} for q in eng}
+    cnt = {q: 0 for q in eng}
+    snap = {}
+    lastw, readers = {}, {}
+
+    def need(q, tok):
+        s, n = tok
+        if clock[q].get(s, 0) >= n:
+            return
+        eng[q].wait_ge(sem[s], n)
+        c = clock[q]
+        for k2, v2 in snap.get(tok, {}).items():
+            if c.get(k2, 0) < v2:
+                c[k2] = v2
+        c[s] = n
+
+    def deps(q, reads, writes, acc=()):
+        own = qsem.get(q)
+        want = {}
+        for k in reads:
+            for t in lastw.get(k, ()):
+                want[t[0]] = max(want.get(t[0], 0), t[1])
+        for k in list(writes) + list(acc):
+            for t in list(lastw.get(k, ())) + list(readers.get(k, ())):
+                if t[0] != own or (k not in acc and t in lastw.get(k, ())):
+                    want[t[0]] = max(want.get(t[0], 0), t[1])
+        for s, n in want.items():
+            need(q, (s, n))
+
+    def op(q, f, reads, writes, acc=()):
+        deps(q, reads, writes, acc)
+        f().then_inc(sem[qsem[q]], 1)
+        cnt[q] += 1
+        tok = (qsem[q], cnt[q])
+        snap[tok] = dict(clock[q])
+        for k in list(writes) + list(acc):
+            lastw[k] = [tok]
+            readers[k] = []
+        for k in reads:
+            readers.setdefault(k, []).append(tok)
+
+    def load(f, name, total, k):
+        f().then_inc(sem[name], 16)
+        lastw[k] = [t for t in lastw.get(k, []) if t[0] != name] + [(name, total)]
+
+    v, pe, act = g.vector, g.tensor, g.scalar
+
+    def ts(out, in0, s1, s2, o0, o1, reads, writes):
+        if o1 is None:
+            op("V", lambda: v.tensor_scalar(out, in0, s1, None, o0), reads, writes)
+        else:
+            op("V", lambda: v.tensor_scalar(out, in0, s1, s2, o0, o1), reads, writes)
+
+    def tt(out, a, b, o, reads, writes):
+        op("V", lambda: v.tensor_tensor(out, a, b, o), reads, writes)
+
+    def cp(out, in_, reads, writes):
+        op("V", lambda: v.tensor_copy(out, in_), reads, writes)
+
+    def ac(out, in_, f, reads, writes, **kw):
+        op("S", lambda: act.activation(out, in_, f, **kw), reads, writes)
+
+    def lin(out, in_, scale, bias, reads, k):
+        ac(out, in_, AF.Copy if isinstance(bias, float) else AF.Identity, reads, [k], scale=scale, bias=bias)
+
+    def mm(out, l, r, start, stop, reads, key):
+        op("P", lambda: pe.matmul(out, l, r, start, stop), reads, (), (key,))
+
+    load(lambda: g.sync.dma_start(T.w0s[:], T.w0[:]), "ldw", 16, "w0s")
+    for gg in range(4):
+        load(lambda: g.sync.dma_start(T.A[16 * gg:16 * gg + 15, N0:N0 + W], T.lk[16 * gg:16 * gg + 15, :]), "ldal", 64, "A")
+    for gg in range(4, 8):
+        load(lambda: act.dma_start(T.A[16 * gg:16 * gg + 15, N0:N0 + W], T.lk[16 * gg:16 * gg + 15, :]), "ldas", 64, "A")
+    load(lambda: g.sync.dma_start(T.A[15::16, N0:N0 + W], T.nx[:]), "ldn", 16, "A")
+    load(lambda: act.dma_start(T.X[:, N0:N0 + W], T.x0[:]), "ldx", 16, "X")
+
+    op("G", lambda: g.iota(T.pI[:], [[0, 1]], 0, 1), [], ["pI"])
+    op("G", lambda: g.iota(T.cI[:], [[1, 256]], 0, 0), [], ["cI"])
+    op("V", lambda: v.memset(T.ZERO[:], 0.0), [], ["ZERO"])
+
+    def stripe(nm, n, cmp, fill, base, step, cm, again=False):
+        op("G", lambda: g.affine_select(T[nm][:], T[nm][:] if again else T.ZERO[:, 0:n], [[step, n]], cmp, fill, base, cm), [nm] if again else ["ZERO"], [nm])
+    stripe("IB", 128, Op.not_equal, 1.0, 0, -1, 1)
+    stripe("IP", 128, Op.not_equal, 2048.0, 0, -1, 1)
+    stripe("IN", 128, Op.not_equal, -2048.0, 0, -1, 1)
+    stripe("WR", 256, Op.not_equal, 63.0 / 128, 0, -1, 1)
+    stripe("WR", 256, Op.not_equal, 63.0 / 128, 128, -1, 1, True)
+    stripe("T2", 128, Op.is_ge, 512.0, 0, 1, -1)
+    op("G", lambda: g.iota(T.cF[:], [[1, 256]], W, 0, allow_small_or_imprecise_dtypes=True), [], ["cF"])
+    op("V", lambda: v.memset(T.X[:, GB:N0], 127.0), [], ["Xd"])
+    op("V", lambda: v.memset(T.A[:, GB:N0], -1), [], ["Ad"])
+    op("V", lambda: v.memset(T.NT0[:, 0:1], 1.0), [], ["NTi0"])
+    op("V", lambda: v.memset(T.NT1[:, 0:1], 1.0), [], ["NTi1"])
+    op("V", lambda: v.memset(T.PW[:], 0.0), [], ["PW"])
+
+    def ci(j): return T.KI[:, j:j + 1]
+    def cf(j): return T.KF[:, j:j + 1]
+    def kk(j): return "KF%d" % j
+    def m16(j): return T.M16[:, j:j + 1]
+    ts(ci(0), T.pI[:], 15, None, Op.bitwise_and, None, ["pI"], ["KI0"])
+    ts(ci(1), T.pI[:], 4, None, Op.arith_shift_right, None, ["pI"], ["KI1"])
+    ts(ci(4), T.pI[:], 1, None, Op.bitwise_and, None, ["pI"], ["KI4"])
+    cp(cf(0), T.pI[:], ["pI"], [kk(0)])
+    cp(cf(1), ci(0), ["KI0"], [kk(1)])
+    cp(cf(2), ci(1), ["KI1"], [kk(2)])
+    ts(ci(5), ci(1), 1, None, Op.bitwise_and, None, ["KI1"], ["KI5"])
+    for j in range(11):
+        op("V", lambda: v.memset(T.PW[:, j::16], 2.0 ** -(j + 1)), ["PW"], ["PWx%d" % j])
+    ts(T.cmI[:], T.cI[:, 0:128], 15, None, Op.bitwise_and, None, ["cI"], ["cmI"])
+    ts(T.cgI[:], T.cI[:, 0:128], 4, None, Op.arith_shift_right, None, ["cI"], ["cgI"])
+    P0, PM, PG = cf(0), cf(1), cf(2)
+    c128 = T.cI[:, 0:128]
+    ts(T.M16[:], T.cI[:, 0:16], PM, None, Op.is_equal, None, ["cI", kk(1)], ["M16"])
+    ts(cf(14), PM, 10.5, -1.5 + 2.0 ** -12, Op.is_lt, Op.mult, [kk(1)], [kk(14)])
+    ts(T.tF[:], T.cmI[:], 14.5, -1.0, Op.is_lt, Op.mult, ["cmI"], ["tF"])
+    ts(T.SAME[:], T.cgI[:], PG, None, Op.is_equal, None, ["cgI", kk(2)], ["SAME"])
+    for nm, f in (("B2", 2.0), ("BN", -1.0), ("B1", 1.0), ("BH", 1.0), ("B4", -4096.0)):
+        ts(T[nm][:], T.cI[:, 0:8], PG, f, Op.is_equal, Op.mult, ["cI", kk(2)], [nm])
+    tt(T.ZM[:], T.tF[:], T.SAME[:], Op.mult, ["tF", "SAME"], ["ZM"])
+    ts(T.DC[:], T.cmI[:], 15, None, Op.is_equal, None, ["cmI"], ["DC"])
+    lin(cf(6), PM, 1.0, -256.0, [kk(1)], kk(6))
+    lin(cf(15), m16(11), 7.5, 1.0, ["M16"], kk(15))
+    lin(cf(13), m16(13), -1.0, 0.0, ["M16"], kk(13))
+    lin(cf(16), m16(13), 126.5, cf(15), ["M16", kk(15)], kk(16))
+    lin(cf(18), cf(16), 1.0, cf(14), [kk(16), kk(14)], kk(18))
+    lin(cf(11), m16(15), 1.0, -1.0, ["M16"], kk(11))
+    lin(cf(12), m16(14), 1.0, -1.0, ["M16"], kk(12))
+    lin(cf(29), m16(12), -11264.0, m16(11), ["M16"], kk(29))
+    lin(cf(28), m16(13), 1.0, m16(15), ["M16"], kk(28))
+    lin(cf(31), cf(29), 1.0, m16(14), ["M16", kk(29)], kk(31))
+    lin(cf(32), cf(28), 512.0, cf(31), [kk(28), kk(31)], kk(32))
+    lin(T.M5[:], T.M16[:], 512.0, 0.0, ["M16"], "M5")
+    lin(T.MN[:], T.M16[:], 1e6, -1e6, ["M16"], "MN")
+    lin(T.AD[:], T.cF[:], m16(14), cf(12), ["cF", "M16", kk(12)], "AD")
+    ts(ci(2), ci(0), -1, 30, Op.mult, Op.add, ["KI0"], ["KI2"])
+    tt(cf(3), P0, PM, Op.subtract, [kk(0), kk(1)], [kk(3)])
+    ts(ci(3), ci(2), 15, None, Op.bitwise_and, None, ["KI2"], ["KI3"])
+    ts(cf(4), PM, 14.5, -2048.0, Op.is_lt, Op.mult, [kk(1)], [kk(4)])
+    tt(cf(5), ci(3), cf(3), Op.add, ["KI3", kk(3)], [kk(5)])
+    ts(T.BLK[:], T.cgI[:], PG, None, Op.is_equal, None, ["cgI", kk(2)], ["BLK"])
+    ts(T.PERM[:], c128, cf(5), None, Op.is_equal, None, ["cI", kk(5)], ["PERM"])
+    ts(T.MK[:], T.cmI[:], PM, None, Op.is_equal, None, ["cmI", kk(1)], ["MK"])
+    ts(cf(7), m16(15), -1000.0, P0, Op.mult, Op.add, ["M16", kk(0)], [kk(7)])
+    ts(T.tF[:], c128, cf(7), 1024.0, Op.is_le, Op.mult, ["cI", kk(7)], ["tF"])
+    tt(T.TRI[:], T.tF[:], T.SAME[:], Op.mult, ["tF", "SAME"], ["TRI"])
+    ts(T.VO[:], T.w0s[:], 8, None, Op.add, None, ["w0s"], ["VO0", "VO1"])
+    cp(T.IH[:], T.IB[:], ["IB"], ["IH"])
+    ts(cf(8), ci(4), 2.0, -1.0, Op.mult, Op.add, ["KI4"], [kk(8)])
+    ts(cf(9), ci(4), -15.0, 15.0, Op.mult, Op.add, ["KI4"], [kk(9)])
+    ts(T.TR[:], T.cI[:, 0:16], 16, cf(6), Op.mult, Op.add, ["cI", kk(6)], ["TR"])
+    ts(cf(19), PM, 10.5, -1.0, Op.is_lt, Op.mult, [kk(1)], [kk(19)])
+    tt(T.WB[:], T.PW[:], T.SAME[:], Op.mult, ["PW", "SAME"] + ["PWx%d" % j for j in range(11)], ["WB"])
+    ts(T.CT[:], T.cI[:], cf(13), cf(18), Op.mult, Op.add, ["cI", kk(13), kk(18)], ["CT"])
+    ts(T.WH[:], T.IB[:], cf(19), None, Op.mult, None, ["IB", kk(19)], ["WH"])
+    ts(T.tF[:], T.cmI[:], 11, -1.0, Op.is_equal, Op.mult, ["cmI"], ["tF"])
+    ts(cf(30), PM, 10.5, 2048.0, Op.is_lt, Op.mult, [kk(1)], [kk(30)])
+    cp(cf(26), ci(5), ["KI5"], [kk(26)])
+    ts(cf(27), ci(5), -1.0, 1.0, Op.mult, Op.add, ["KI5"], [kk(27)])
+    tt(T.WC[:], T.tF[:], T.SAME[:], Op.mult, ["tF", "SAME"], ["WC"])
+    for (base, par) in ((20, 27), (23, 26)):
+        ts(T.KF[:, base:base + 3], T.KF[:, 30:33], cf(par), None, Op.mult, None, [kk(30), kk(31), kk(32), kk(par)], [kk(base)])
+
+    def buf(n, b): return T[n + "%d" % b]
+    def key(n, b): return "%s%d" % (n, b)
+    def xread(t): return ["X", "Xd"] + (["Xown0", "Xarr0"] if t else [])
+    def xwin(t): return T.X[:, GB:N0 + W + K * t]
+    def awin(t): return T.A[:, GB:N0 + W + K * t]
+    def vo(b): return T.VO[:, 8 * b:8 * b + 8]
+    def wb(b): return slice(128 * b, 128 * b + 128)
+
+    def links(t, b):
+        op("V", lambda: v.tensor_scalar(buf("AO", b)[:], awin(t).indirect(vo(b)), 8, None, Op.add),
+           ["A", "Ad", "Anew0", "Anew1", key("VO", b)], [key("AO", b)])
+
+    def numbers(t, b, hs=(0, 1)):
+        for h in hs:
+            ac(buf("D", b)[:, 1024 * h:1024 * h + 1024], xwin(t).indirect(buf("AO", b)[:, 64 * h:64 * h + 64]), AF.Copy,
+               [key("AO", b)] + xread(t), ["D%d%d" % (b, h)])
+
+    def half(b):
+        cp(buf("AH", b)[:], buf("AO", b)[:], [key("AO", b)], [key("AH", b)])
+
+    def gather_y(t, b):
+        cp(T.Y[:, wb(b)], xwin(t).indirect(vo(b)), [key("VO", b)] + xread(t), [key("Y", b)])
+
+    def halve(b):
+        o = buf("ch", b)[:, 384:512]
+        mm(o, T.WR[:, 0:128], buf("Z", b)[:], True, False, ["WR", key("Z", b)], key("ch", b))
+        mm(o, T.WR[:, 0:128], T.Y[:, wb(b)], False, True, ["WR", key("Y", b)], key("ch", b))
+
+    def new_z(b):
+        ts(buf("Z", b)[:], buf("ch", b)[:, 384:512], MAGIC, MAGIC, Op.add, Op.subtract, [key("ch", b)], [key("Z", b)])
+
+    def spread_z(b):
+        for r in range(KZ):
+            mm(buf("zp", b)[:, r::KZ], T.IB[:], buf("Z", b)[:], True, True, ["IB", key("Z", b)], key("zp", b))
+        mm(buf("dist", b)[:, 0:128], buf("Z", b)[:], T.ZM[:], True, False, ["ZM", key("Z", b)], key("dist", b))
+
+    def bar(b, k):
+        for k2 in range(k):
+            mm(buf("dist", b)[:, 0:128], buf("SA", b)[:, wb(k2)], T.TRI[:], False, False, ["TRI", key("SA", b)], key("dist", b))
+
+    def sums_d(t, b):
+        for i in range(15):
+            w = T.B1 if (t == 0 and i == 14) else T.BN
+            mm(buf("dist", b)[:, 14 - i:128:16], buf("D", b)[:, i::16], w[:], False, False, ["B1", "BN", "D%d0" % b, "D%d1" % b], key("dist", b))
+
+    PLAN = [[[(0, 4)], [(1, 4)], [(2, 8), (6, 16)], [(3, 8), (7, 16)]], [[(0, 4)], [(1, 4)], [(2, 4)], [(3, 8), (7, 16)]]]
+
+    def max_op(t, b, h, j):
+        for (a, st) in PLAN[t][j]:
+            r = slice(1024 * h + a, 1024 * h + 1024, st)
+            tt(buf("M", b)[:, r], buf("D", b)[:, r], buf("zp", b)[:, 256 * h:256 * h + 256:st // 4], Op.max, ["D%d%d" % (b, h), key("zp", b)], ["M%d%d%d" % (b, h, a)])
+
+    def sums_m(t, b, j):
+        for (a, st) in PLAN[t][j]:
+            for i in range(a, 16, st):
+                mm(buf("dist", b)[:, 14 - i:128:16], buf("M", b)[:, i::16], T.B2[:], False, i == 7,
+                   ["B2", "M%d0%d" % (b, a), "M%d1%d" % (b, a)], key("dist", b))
+
+    def sel_a(b):
+        ts(buf("NV", b)[:], buf("dist", b)[:, 0:128], 65.5, None, Op.is_ge, None, [key("dist", b)], [key("NV", b)])
+        op("V", lambda: v.tensor_tensor_scan(buf("NT", b)[:, 1:129], buf("NV", b)[:], T.DC[:], 1.0, Op.mult, Op.max), [key("NV", b), "DC"], [key("NT", b)])
+        o = buf("ch", b)[:, 0:128]
+        mm(o, T.PERM[:], buf("AH", b)[:], True, False, ["PERM", key("AH", b)], key("ch", b))
+        mm(o, buf("NT", b)[:, 0:128], T.IP[:], False, False, ["IP", key("NTi", b), key("NT", b)], key("ch", b))
+        mm(o, buf("NT", b)[:, 1:129], T.IN[:], False, True, ["IN", key("NT", b)], key("ch", b))
+
+    def sel_b(b, k):
+        sa = buf("SA", b)[:, wb(k)]
+        ts(sa, buf("ch", b)[:, 0:128], cf(4), 0.0, Op.add, Op.max, [key("ch", b), kk(4)], [key("SA", b)])
+        mm(buf("ch", b)[:, 128:256], sa, T.BLK[:], True, True, ["BLK", key("SA", b)], key("ch", b))
+
+    def sel_c(b):
+        tt(buf("LT", b)[:], buf("ch", b)[:, 128:256], T.MK[:], Op.mult, [key("ch", b), "MK"], [key("LT", b)])
+        mm(buf("ch", b)[:, 256:264], buf("LT", b)[:], T.BH[:], True, True, ["BH", key("LT", b)], key("ch", b))
+
+    def sel_d(b):
+        cp(vo(b), buf("ch", b)[:, 256:264], [key("ch", b)], [key("VO", b)])
+
+    def bits1(b):
+        for lo in (128, 256):
+            o = buf("dist", b)[:, lo:lo + 128]
+            mm(o, T.IH[:], T.CT[:, wb(b)], True, False, ["IH", "CT"], key("dist", b))
+            mm(o, T.WB[:], buf("SA", b)[:, wb(4)], False, lo == 128, ["WB", key("SA", b)], key("dist", b))
+
+    def bits2(b):
+        ts(buf("HH", b)[:], buf("dist", b)[:, 128:256], MAGIC, MAGIC, Op.add, Op.subtract, [key("dist", b)], [key("HH", b)])
+
+    def vote(b):
+        tt(T.GT[:, wb(b)], T.Y[:, wb(b)], buf("zp", b)[:, 0::KZ], Op.is_gt, [key("Y", b), key("zp", b)], [key("GT", b)])
+        o = buf("dist", b)[:, 256:384]
+        mm(o, T.WH[:], buf("HH", b)[:], False, False, ["WH", key("HH", b)], key("dist", b))
+        mm(o, T.WC[:], T.GT[:, wb(b)], False, True, ["WC", key("GT", b)], key("dist", b))
+
+    def bits3(b):
+        ts(T.RB[:, wb(b)], buf("dist", b)[:, 256:384], 0.0, 0.5, Op.is_gt, Op.subtract, [key("dist", b)], [key("RB", b)])
+
+    def left(b, q):
+        for (nm, base) in (("LE", 20), ("LO", 23)):
+            if q == "V":
+                ts(T[nm][:, wb(b)], T.RB[:, wb(b)], cf(base), cf(base + 1 + b), Op.mult, Op.add, [key("RB", b), kk(base)], [key(nm, b)])
+            else:
+                ac(T[nm][:, wb(b)], T.RB[:, wb(b)], AF.Identity, [key("RB", b), kk(base)], [key(nm, b)], scale=cf(base), bias=cf(base + 1 + b))
+
+    def flipped(b):
+        ac(T.FY[:, wb(b)], T.Y[:, wb(b)], AF.Identity, [key("Y", b), kk(8), kk(9)], [key("FY", b)], scale=cf(8), bias=cf(9))
+
+    def turn(b):
+        for j in range(4):
+            d = (4 * b + j - rank) % 8
+            rot = T.WR[:, 128 - 16 * d:256 - 16 * d]
+            oo = buf("ch", b)[:, 384 + 32 * j:416 + 32 * j]
+            mm(oo, rot, buf("Z", b)[:, 32 * j:32 * j + 32], True, False, ["WR", key("Z", b)], key("ch", b))
+            mm(oo, rot, T.Y[:, 128 * b + 32 * j:128 * b + 32 * j + 32], False, True, ["WR", key("Y", b)], key("ch", b))
+
+    sent = [0]
+
+    def send(t, b):
+        zs, o = T["ZS%d" % t], buf("ch", b)
+        c0 = N0 + W + K * t + 32 * rank
+        ts(zs[:, wb(b)], o[:, 384:512], MAGIC, MAGIC, Op.add, Op.subtract, [key("ch", b)], ["ZS%d%d" % (t, b)])
+        if rank // 4 == b:
+            j = rank % 4
+            ts(T.X[:, c0:c0 + 32], o[:, 384 + 32 * j:416 + 32 * j], MAGIC, MAGIC, Op.add, Op.subtract, [key("ch", b)], ["Xown%d" % t])
+        deps("G", ["ZS%d%d" % (t, b)], [])
+        trs, used = [], set()
+        for q in sorted([q for q in range(4 * b, 4 * b + 4) if q != rank], key=lambda q: len(topo.engines(core, T.cores[q]))):
+            dst = T.cores[q]
+            es = topo.engines(core, dst)
+            es = es[0::2] + es[1::2]
+            if dst in topo.cores_of(core):
+                es = es[::-1]
+            e = [x for x in es if x not in used][0]
+            used.add(e)
+            rid, pid = topo.addr(dst, core)
+            trs.append(RemoteDMATransfer(dst_ids=[DstId(rid=rid, pnc=pid)], dma_engine_mask=1 << e, remote_sem=sem["arr%d" % t],
+                                         src=zs[:, 32 * q:32 * q + 32], dst=T.X[:, c0:c0 + 32]))
+        g.remote_dma_fused(trs, local_sem=sem["snt"])
+        sent[0] += len(trs)
+
+    def pairs(bk, lo, gg, c, first, last, kb):
+        a, nm = gg // 2, "LE" if gg % 2 == 0 else "LO"
+        tri = first <= 128 * c < last
+        mm(bk[:, lo:lo + last - first], T[nm][32 * a:32 * a + 32, wb(c)], T.RB[32 * a:32 * a + 32, first:last], True, not tri,
+           [key(nm, c), "RB0"] + (["RB1"] if last > 128 else []), kb)
+        if tri:
+            mm(bk[:, lo + 128 * c - first:lo + 128 * c - first + 128], T.IB[:], T.T2[:], False, True, ["IB", "T2"], kb)
+
+    def reduce_v(src, j, kb):
+        op("V", lambda: v.tensor_reduce(T.ACV[:, j:j + 1], src, AxisListType.X, Op.max), [kb], ["ACV%d" % j])
+
+    def reduce_s(src, n, j, kb):
+        o = 256 * (j % 4)
+        ac(T.junk[:, o:o + n], src, AF.Relu, [kb], ["ACS%d" % j, "junk%d" % (j % 4)], accum_out=T.ACS[:, j:j + 1])
+
+    def place_v(nm, gg, j, an):
+        ts(T[nm][:, 16 * gg:16 * gg + 16], T.M5[:], T[an][:, j:j + 1], 0.0, Op.min, Op.max, ["M5", "%s%d" % (an, j)], ["%s%d" % (nm, gg)])
+
+    def place_s(nm, gg, j):
+        ac(T[nm][:, 16 * gg:16 * gg + 16], T.MN[:], AF.Relu, ["MN", "ACS%d" % j], ["%s%d" % (nm, gg)], bias=T.ACS[:, j:j + 1])
+
+    def early(gs):
+        kbs = ["eA", "eB", "dist0", "zp0"]
+        for gg in gs:
+            pairs(T[kbs[gg // 2]], 128 * (gg % 2), gg, 0, 0, 128, kbs[gg // 2])
+        for gg in gs:
+            reduce_s(T[kbs[gg // 2]][:, 128 * (gg % 2):128 * (gg % 2) + 128], 128, gg, kbs[gg // 2])
+
+    def new_links(t, b):
+        op("V", lambda: v.tensor_tensor(T.VAL[:, wb(b)], awin(t).indirect(vo(b)), T.AD[:, wb(b)], Op.max), ["A", "Ad", key("VO", b), "AD"], [key("VAL", b)])
+
+    def new_nodes(b):
+        ts(T.A[:, N0 + W + 128 * b:N0 + W + 128 * b + 128], T.VAL[:, wb(b)], m16(15), cf(11), Op.mult, Op.add, [key("VAL", b), "M16", kk(11)], [key("Anew", b)])
+
+    def final_nodes(b):
+        mm(buf("ch", b)[:, 128:256], T.BLK[:], buf("SA", b)[:, wb(4)], True, True, ["BLK", key("SA", b)], key("ch", b))
+        ts(T.YV[:, wb(b)], buf("ch", b)[:, 128:256], 8.0, None, Op.subtract, None, [key("ch", b)], [key("YV", b)])
+
+    def late(t):
+        banks = [("eA", T.eA), ("eB", T.eB), ("dist0", T.dist0), ("dist1", T.dist1)]
+        extra = [lambda: new_links(t, 0), lambda: new_links(t, 1), lambda: new_nodes(0), lambda: new_nodes(1)] if t == 0 else [lambda: final_nodes(0), lambda: final_nodes(1)]
+        for p in range(4):
+            for gg in (2 * p, 2 * p + 1):
+                kb, bk = banks[gg % 4]
+                pairs(bk, 0, gg, 0, 128, 256, kb)
+                pairs(bk, 256, gg, 1, 0, 256, kb)
+            if t == 0 or p < 2:
+                extra[p]()
+            for gg in (2 * p, 2 * p + 1):
+                kb, bk = banks[gg % 4]
+                if gg in (1, 3, 4, 6):
+                    reduce_s(bk[:, 0:128], 128, 8 + 2 * gg, kb)
+                    reduce_s(bk[:, 256:512], 256, 9 + 2 * gg, kb)
+                    place_s("LAB", gg, 8 + 2 * gg)
+                    place_s("LBB", gg, 9 + 2 * gg)
+                else:
+                    reduce_v(bk[:, 0:128], 2 * gg, kb)
+                    reduce_v(bk[:, 256:512], 2 * gg + 1, kb)
+                    place_v("LAB", gg, 2 * gg, "ACV")
+                    place_v("LBB", gg, 2 * gg + 1, "ACV")
+        ra, rb, rc = [["%s%d" % (nm, gg) for gg in range(8)] for nm in ("LAA", "LAB", "LBB")]
+        for (lo, w, wn) in (((256, T.B1, "B1"),) if t == 0 else ()) + ((288, T.B4, "B4"),):
+            oa, ob = T.ch0[:, lo:lo + 8], T.ch0[:, lo + 8:lo + 16]
+            isx = wn == "B4"
+            if isx:
+                mm(oa, T.LT0[:], T.BH[:], True, False, ["BH", "LT0"], "ch0")
+            mm(oa, T.LAA[:], w[:], not isx, False, [wn] + ra, "ch0")
+            mm(oa, T.LAB[:], w[:], False, True, [wn] + rb, "ch0")
+            if isx:
+                mm(ob, T.LT1[:], T.BH[:], True, False, ["BH", "LT1"], "ch0")
+            mm(ob, T.LBB[:], w[:], not isx, True, [wn] + rc, "ch0")
+        if t == 0:
+            ts(T.FR[:], T.ch0[:, 256:272], 511.5, -4096.0, Op.is_ge, Op.mult, ["ch0"], ["FR"])
+        tt(T.FF[:], T.ch0[:, 288:304], T.TR[:], Op.max, ["ch0", "TR"], ["FF"])
+        if t == 0:
+            tt(T.FR[:], T.FR[:], T.DV[:], Op.add, ["FR", "DV"], ["FR"])
+        ts(T.OFX[:], T.FF[:], float(GB), None, Op.add, None, ["FF"], ["OFX"])
+        if t == 0:
+            tt(T.FR[:], T.FR[:], T.TR[:], Op.max, ["FR", "TR"], ["FR"])
+            ts(T.OFA[:], T.FR[:], float(GB), None, Op.add, None, ["FR"], ["OFA"])
+            cp(T.A[:, 0:N0 + W].indirect(T.OFA[:]), T.VAL[:], ["OFA", "VAL0", "VAL1", "Ad"], ["A"])
+
+    def flip(t):
+        cp(T.X[:, 0:N0 + W + K * t].indirect(T.OFX[:]), T.FY[:], ["OFX", "FY0", "FY1", "Xd"] + (["Xown0", "Xarr0"] if t else []), ["X"])
+
+    for t in range(RO):
+        lastw["Xarr%d" % t] = [("arr%d" % t, 7)]
+        links(t, 0)
+        if t:
+            flip(0)
+        numbers(t, 0, (1,))
+        links(t, 1)
+        numbers(t, 1)
+        for b in range(2):
+            cp(buf("Z", b)[:], xwin(t).indirect(vo(b)), [key("VO", b)] + xread(t), [key("Z", b)])
+            spread_z(b)
+            if b == 0:
+                cp(T.D0[:, 0:1024], xwin(t).indirect(T.AO0[:, 0:64]), ["AO0"] + xread(t), ["D00"])
+        half(0)
+        half(1)
+        for j in range(4):
+            max_op(t, 0, 0, j)
+        barred = None
+        for k in range(S):
+            for b in range(2):
+                last = (b, k) == (1, S - 1)
+                nb = 1 - b
+
+                def fill(j):
+                    if not last:
+                        max_op(t, nb, 0, j)
+                sums_d(t, b)
+                if last:
+                    bits2(0)
+                for j in range(4):
+                    max_op(t, b, 1, j)
+                    sums_m(t, b, j)
+                sel_a(b)
+                if barred is not None:
+                    bar(*barred)
+                    barred = None
+                if last:
+                    vote(0)
+                fill(0)
+                sel_b(b, k)
+                if last:
+                    turn(0)
+                    bits1(1)
+                    bits3(0)
+                    left(0, "S")
+                    flipped(0)
+                fill(1)
+                sel_c(b)
+                if last:
+                    send(t, 0)
+                    bits2(1)
+                    early(range(0, 4))
+                fill(2)
+                sel_d(b)
+                if k < S - 1:
+                    gather_y(t, b)
+                    halve(b)
+                    links(t, b)
+                    numbers(t, b)
+                    new_z(b)
+                    fill(3)
+                    spread_z(b)
+                    half(b)
+                    barred = (b, k + 1)
+                elif b == 0:
+                    bits1(0)
+                    ac(T.Y[:, wb(0)], xwin(t).indirect(vo(0)), AF.Copy, ["VO0"] + xread(t), ["Y0"])
+                    fill(3)
+                else:
+                    gather_y(t, 1)
+                    vote(1)
+                    bits3(1)
+                    left(1, "V")
+                    early(range(4, 8))
+                    turn(1)
+                    flipped(1)
+                    if t == 0:
+                        ts(T.DV[:], T.VO[:], 1.0, None, Op.mult, None, ["VO0", "VO1"], ["DV"])
+                    send(t, 1)
+                    for gg in range(8):
+                        place_v("LAA", gg, gg, "ACS")
+                    late(t)
+    flip(RO - 1)
+    deps("S", ["X", "Xd", "Xown0", "Xarr0"], [])
+    act.dma_start(T.yx[:, 0:W + K], T.X[:, N0:N0 + W + K]).then_inc(sem.out2, 16)
+    deps("Y", ["YV0", "YV1"], [])
+    g.sync.dma_start(T.yv[:], T.YV[0::16, :]).then_inc(sem.out1, 16)
+    deps("Y", ["Xown1", "Xarr1"], [])
+    g.sync.dma_start(T.yx[:, W + K:W + 2 * K], T.X[:, N0 + W + K:N0 + W + 2 * K]).then_inc(sem.out3, 16)
+    for s, n in (("qV", cnt["V"]), ("qP", cnt["P"]), ("qS", cnt["S"]), ("qG", cnt["G"]), ("snt", sent[0]), ("arr0", 7), ("arr1", 7),
+                 ("out1", 16), ("out2", 16), ("out3", 16), ("ldw", 16), ("ldx", 16), ("ldal", 64), ("ldas", 64), ("ldn", 16)):
+        g.wait_ge(sem[s], n)

@@ -158,8 +158,6 @@ def rank_program(g, core, T, topo):
     cp(cf(1), ci(0), ["KI0"], [kk(1)])
     cp(cf(2), ci(1), ["KI1"], [kk(2)])
     ts(ci(5), ci(1), 1, None, Op.bitwise_and, None, ["KI1"], ["KI5"])
-    for j in range(11):
-        op("V", lambda: v.memset(T.PW[:, j::16], 2.0 ** -(j + 1)), ["PW"], ["PWx%d" % j])
     ts(T.cmI[:], T.cI[:, 0:128], 15, None, Op.bitwise_and, None, ["cI"], ["cmI"])
     ts(T.cgI[:], T.cI[:, 0:128], 4, None, Op.arith_shift_right, None, ["cI"], ["cgI"])
     P0, PM, PG = cf(0), cf(1), cf(2)
@@ -198,21 +196,27 @@ def rank_program(g, core, T, topo):
     ts(T.tF[:], c128, cf(7), 1024.0, Op.is_le, Op.mult, ["cI", kk(7)], ["tF"])
     tt(T.TRI[:], T.tF[:], T.SAME[:], Op.mult, ["tF", "SAME"], ["TRI"])
     ts(T.VO[:], T.w0s[:], 8, None, Op.add, None, ["w0s"], ["VO0", "VO1"])
-    cp(T.IH[:], T.IB[:], ["IB"], ["IH"])
-    ts(cf(8), ci(4), 2.0, -1.0, Op.mult, Op.add, ["KI4"], [kk(8)])
-    ts(cf(9), ci(4), -15.0, 15.0, Op.mult, Op.add, ["KI4"], [kk(9)])
-    ts(T.TR[:], T.cI[:, 0:16], 16, cf(6), Op.mult, Op.add, ["cI", kk(6)], ["TR"])
-    ts(cf(19), PM, 10.5, -1.0, Op.is_lt, Op.mult, [kk(1)], [kk(19)])
-    tt(T.WB[:], T.PW[:], T.SAME[:], Op.mult, ["PW", "SAME"] + ["PWx%d" % j for j in range(11)], ["WB"])
-    ts(T.CT[:], T.cI[:], cf(13), cf(18), Op.mult, Op.add, ["cI", kk(13), kk(18)], ["CT"])
-    ts(T.WH[:], T.IB[:], cf(19), None, Op.mult, None, ["IB", kk(19)], ["WH"])
-    ts(T.tF[:], T.cmI[:], 11, -1.0, Op.is_equal, Op.mult, ["cmI"], ["tF"])
-    ts(cf(30), PM, 10.5, 2048.0, Op.is_lt, Op.mult, [kk(1)], [kk(30)])
-    cp(cf(26), ci(5), ["KI5"], [kk(26)])
-    ts(cf(27), ci(5), -1.0, 1.0, Op.mult, Op.add, ["KI5"], [kk(27)])
-    tt(T.WC[:], T.tF[:], T.SAME[:], Op.mult, ["tF", "SAME"], ["WC"])
+    deferred = []
+
+    def later(f, *a):
+        deferred.append(lambda: f(*a))
+    later(cp, T.IH[:], T.IB[:], ["IB"], ["IH"])
+    later(ts, cf(8), ci(4), 2.0, -1.0, Op.mult, Op.add, ["KI4"], [kk(8)])
+    later(ts, cf(9), ci(4), -15.0, 15.0, Op.mult, Op.add, ["KI4"], [kk(9)])
+    later(ts, T.TR[:], T.cI[:, 0:16], 16, cf(6), Op.mult, Op.add, ["cI", kk(6)], ["TR"])
+    later(ts, cf(19), PM, 10.5, -1.0, Op.is_lt, Op.mult, [kk(1)], [kk(19)])
+    for j in range(11):
+        later(op, "V", lambda j=j: v.memset(T.PW[:, j::16], 2.0 ** -(j + 1)), ["PW"], ["PWx%d" % j])
+    later(tt, T.WB[:], T.PW[:], T.SAME[:], Op.mult, ["PW", "SAME"] + ["PWx%d" % j for j in range(11)], ["WB"])
+    later(ts, T.CT[:], T.cI[:], cf(13), cf(18), Op.mult, Op.add, ["cI", kk(13), kk(18)], ["CT"])
+    later(ts, T.WH[:], T.IB[:], cf(19), None, Op.mult, None, ["IB", kk(19)], ["WH"])
+    later(ts, T.tF[:], T.cmI[:], 11, -1.0, Op.is_equal, Op.mult, ["cmI"], ["tF"])
+    later(ts, cf(30), PM, 10.5, 2048.0, Op.is_lt, Op.mult, [kk(1)], [kk(30)])
+    later(cp, cf(26), ci(5), ["KI5"], [kk(26)])
+    later(ts, cf(27), ci(5), -1.0, 1.0, Op.mult, Op.add, ["KI5"], [kk(27)])
+    later(tt, T.WC[:], T.tF[:], T.SAME[:], Op.mult, ["tF", "SAME"], ["WC"])
     for (base, par) in ((20, 27), (23, 26)):
-        ts(T.KF[:, base:base + 3], T.KF[:, 30:33], cf(par), None, Op.mult, None, [kk(30), kk(31), kk(32), kk(par)], [kk(base)])
+        later(ts, T.KF[:, base:base + 3], T.KF[:, 30:33], cf(par), None, Op.mult, None, [kk(30), kk(31), kk(32), kk(par)], [kk(base)])
 
     def buf(n, b): return T[n + "%d" % b]
     def key(n, b): return "%s%d" % (n, b)
@@ -383,8 +387,6 @@ def rank_program(g, core, T, topo):
 
     def new_links(t, b):
         op("V", lambda: v.tensor_tensor(T.VAL[:, wb(b)], awin(t).indirect(vo(b)), T.AD[:, wb(b)], Op.max), ["A", "Ad", key("VO", b), "AD"], [key("VAL", b)])
-
-    def new_nodes(b):
         ts(T.A[:, N0 + W + 128 * b:N0 + W + 128 * b + 128], T.VAL[:, wb(b)], m16(15), cf(11), Op.mult, Op.add, [key("VAL", b), "M16", kk(11)], [key("Anew", b)])
 
     def final_nodes(b):
@@ -393,14 +395,13 @@ def rank_program(g, core, T, topo):
 
     def late(t):
         banks = [("eA", T.eA), ("eB", T.eB), ("dist0", T.dist0), ("dist1", T.dist1)]
-        extra = [lambda: new_links(t, 0), lambda: new_links(t, 1), lambda: new_nodes(0), lambda: new_nodes(1)] if t == 0 else [lambda: final_nodes(0), lambda: final_nodes(1)]
         for p in range(4):
             for gg in (2 * p, 2 * p + 1):
                 kb, bk = banks[gg % 4]
                 pairs(bk, 0, gg, 0, 128, 256, kb)
                 pairs(bk, 256, gg, 1, 0, 256, kb)
-            if t == 0 or p < 2:
-                extra[p]()
+            if t and p < 2:
+                final_nodes(p)
             for gg in (2 * p, 2 * p + 1):
                 kb, bk = banks[gg % 4]
                 if gg in (1, 3, 4, 6):
@@ -455,28 +456,35 @@ def rank_program(g, core, T, topo):
         half(1)
         for j in range(4):
             max_op(t, 0, 0, j)
-        barred = None
+        pend = None
         for k in range(S):
             for b in range(2):
                 last = (b, k) == (1, S - 1)
                 nb = 1 - b
 
-                def fill(j):
-                    if not last:
-                        max_op(t, nb, 0, j)
+                def fill(*js):
+                    for j in js:
+                        if not last:
+                            max_op(t, nb, 0, j)
                 sums_d(t, b)
                 if last:
                     bits2(0)
                 for j in range(4):
                     max_op(t, b, 1, j)
                     sums_m(t, b, j)
+                if pend:
+                    gather_y(t, nb)
+                    halve(nb)
+                    half(nb)
                 sel_a(b)
-                if barred is not None:
-                    bar(*barred)
-                    barred = None
+                if pend:
+                    new_z(nb)
+                    spread_z(nb)
                 if last:
                     vote(0)
-                fill(0)
+                for f in deferred[:4]:
+                    f()
+                del deferred[:4]
                 sel_b(b, k)
                 if last:
                     turn(0)
@@ -484,24 +492,24 @@ def rank_program(g, core, T, topo):
                     bits3(0)
                     left(0, "S")
                     flipped(0)
-                fill(1)
+                    if t == 0:
+                        new_links(t, 0)
+                fill(0)
                 sel_c(b)
                 if last:
                     send(t, 0)
                     bits2(1)
                     early(range(0, 4))
-                fill(2)
+                fill(1, 2)
+                if pend:
+                    bar(*pend)
+                pend = None
                 sel_d(b)
                 if k < S - 1:
-                    gather_y(t, b)
-                    halve(b)
                     links(t, b)
                     numbers(t, b)
-                    new_z(b)
+                    pend = (b, k + 1)
                     fill(3)
-                    spread_z(b)
-                    half(b)
-                    barred = (b, k + 1)
                 elif b == 0:
                     bits1(0)
                     ac(T.Y[:, wb(0)], xwin(t).indirect(vo(0)), AF.Copy, ["VO0"] + xread(t), ["Y0"])
@@ -517,6 +525,8 @@ def rank_program(g, core, T, topo):
                     if t == 0:
                         ts(T.DV[:], T.VO[:], 1.0, None, Op.mult, None, ["VO0", "VO1"], ["DV"])
                     send(t, 1)
+                    if t == 0:
+                        new_links(t, 1)
                     for gg in range(8):
                         place_v("LAA", gg, gg, "ACS")
                     late(t)

import numpy as np
from concourse.bass import DstId, RemoteDMATransfer
from concourse.mybir import dt, AluOpType as Op, AxisListType, ActivationFunctionType as AF

W, K, RO, S = 1664, 256, 2, 5
GB = 256
N0 = GB + 8
XC = N0 + W + RO * K
AC = N0 + W + K
MAGIC = 12582912.0
KZ = 4

SCRATCH = {}


def declare(where, dtype, names, shape):
    for nm in names.split():
        SCRATCH[nm] = (where, shape, dtype)


declare("sbuf", "bfloat16", "X", [128, XC])
declare("sbuf", "int32", "A", [128, AC])
declare("sbuf", "int32", "w0s KI", [128, 16])
declare("sbuf", "uint16", "VO OFX OFA", [128, 16])
declare("sbuf", "bfloat16", "Y GT FY RB LE LO ZS0 ZS1 ZERO WR", [128, 256])
declare("sbuf", "bfloat16", "junk", [128, 1024])
declare("sbuf", "float32", "VAL YV AD cF", [128, 256])
declare("sbuf", "float32", "ACV DV FF FR M16 M5 MN TR", [128, 16])
declare("sbuf", "float32", "ACS", [128, 32])
declare("sbuf", "float32", "KF", [128, 40])
declare("sbuf", "bfloat16", "LAA LAB LBB IB IP IN ZM MK DC WC T2 Z0 Z1 NV0 NV1", [128, 128])
declare("sbuf", "float16", "IH TRI PERM BLK WB WH AH0 AH1 LT0 LT1 HH0 HH1", [128, 128])
declare("sbuf", "float32", "tF SAME PW", [128, 128])
declare("sbuf", "int32", "cmI cgI", [128, 128])
declare("sbuf", "int32", "cI", [128, 256])
declare("sbuf", "int32", "pI", [128, 1])
declare("sbuf", "bfloat16", "B2 BN B1 B4", [128, 8])
declare("sbuf", "float16", "BH", [128, 8])
declare("sbuf", "float16", "CT", [128, 256])
declare("sbuf", "bfloat16", "D0 D1 M0 M1", [128, 2048])
declare("sbuf", "uint16", "AO0 AO1", [128, 128])
declare("sbuf", "bfloat16", "NT0 NT1", [128, 136])
declare("sbuf", "float16", "SA0 SA1", [128, S * 128])
declare("psum", "float32", "eA eB dist0 dist1 ch0 ch1 zp0 zp1", [128, 512])
SEMAPHORES = ["qV", "qP", "qS", "qG", "ldw", "ldx", "ldal", "ldas", "ldn", "arr0", "arr1", "snt", "out1", "out2", "out3"]


def rank_program(g, core, T, topo):
    rank = T.rank_of(core)
    if rank is None:
        return
    sem = T.sem
    eng = {"V": g.vector, "P": g.tensor, "S": g.scalar, "G": g, "Y": g.sync}
    qsem = {"V": "qV", "P": "qP", "S": "qS", "G": "qG"}
    clock = {q: {} for q in eng}
    cnt = {q: 0 for q in eng}
    snap = {}
    lastw, readers = {}, {}

    def need(q, tok):
        s, n = tok
        if clock[q].get(s, 0) >= n:
            return
        eng[q].wait_ge(sem[s], n)
        c = clock[q]
        for k2, v2 in snap.get(tok, {}).items():
            if c.get(k2, 0) < v2:
                c[k2] = v2
        c[s] = n

    def deps(q, reads, writes, acc=()):
        own = qsem.get(q)
        want = {}
        for k in reads:
            for t in lastw.get(k, ()):
                want[t[0]] = max(want.get(t[0], 0), t[1])
        for k in list(writes) + list(acc):
            for t in list(lastw.get(k, ())) + list(readers.get(k, ())):
                if t[0] != own or (k not in acc and t in lastw.get(k, ())):
                    want[t[0]] = max(want.get(t[0], 0), t[1])
        for s, n in want.items():
            need(q, (s, n))

    def op(q, f, reads, writes, acc=()):
        deps(q, reads, writes, acc)
        f().then_inc(sem[qsem[q]], 1)
        cnt[q] += 1
        tok = (qsem[q], cnt[q])
        snap[tok] = dict(clock[q])
        for k in list(writes) + list(acc):
            lastw[k] = [tok]
            readers[k] = []
        for k in reads:
            readers.setdefault(k, []).append(tok)

    def load(f, name, total, k):
        f().then_inc(sem[name], 16)
        lastw[k] = [t for t in lastw.get(k, []) if t[0] != name] + [(name, total)]

    v, pe, act = g.vector, g.tensor, g.scalar

    def ts(out, in0, s1, s2, o0, o1, reads, writes):
        if o1 is None:
            op("V", lambda: v.tensor_scalar(out, in0, s1, None, o0), reads, writes)
        else:
            op("V", lambda: v.tensor_scalar(out, in0, s1, s2, o0, o1), reads, writes)

    def tt(out, a, b, o, reads, writes):
        op("V", lambda: v.tensor_tensor(out, a, b, o), reads, writes)

    def cp(out, in_, reads, writes):
        op("V", lambda: v.tensor_copy(out, in_), reads, writes)

    def ac(out, in_, f, reads, writes, **kw):
        op("S", lambda: act.activation(out, in_, f, **kw), reads, writes)

    def lin(out, in_, scale, bias, reads, k):
        ac(out, in_, AF.Copy if isinstance(bias, float) else AF.Identity, reads, [k], scale=scale, bias=bias)

    def mm(out, l, r, start, stop, reads, key):
        op("P", lambda: pe.matmul(out, l, r, start, stop), reads, (), (key,))

    load(lambda: g.sync.dma_start(T.w0s[:], T.w0[:]), "ldw", 16, "w0s")
    for gg in range(4):
        load(lambda: g.sync.dma_start(T.A[16 * gg:16 * gg + 15, N0:N0 + W], T.lk[16 * gg:16 * gg + 15, :]), "ldal", 64, "A")
    for gg in range(4, 8):
        load(lambda: act.dma_start(T.A[16 * gg:16 * gg + 15, N0:N0 + W], T.lk[16 * gg:16 * gg + 15, :]), "ldas", 64, "A")
    load(lambda: g.sync.dma_start(T.A[15::16, N0:N0 + W], T.nx[:]), "ldn", 16, "A")
    load(lambda: act.dma_start(T.X[:, N0:N0 + W], T.x0[:]), "ldx", 16, "X")

    op("G", lambda: g.iota(T.pI[:], [[0, 1]], 0, 1), [], ["pI"])
    op("G", lambda: g.iota(T.cI[:], [[1, 256]], 0, 0), [], ["cI"])
    op("V", lambda: v.memset(T.ZERO[:], 0.0), [], ["ZERO"])

    def stripe(nm, n, cmp, fill, base, step, cm, again=False):
        op("G", lambda: g.affine_select(T[nm][:], T[nm][:] if again else T.ZERO[:, 0:n], [[step, n]], cmp, fill, base, cm), [nm] if again else ["ZERO"], [nm])
    stripe("IB", 128, Op.not_equal, 1.0, 0, -1, 1)
    stripe("IP", 128, Op.not_equal, 2048.0, 0, -1, 1)
    stripe("IN", 128, Op.not_equal, -2048.0, 0, -1, 1)
    stripe("WR", 256, Op.not_equal, 63.0 / 128, 0, -1, 1)
    stripe("WR", 256, Op.not_equal, 63.0 / 128, 128, -1, 1, True)
    stripe("T2", 128, Op.is_ge, 512.0, 0, 1, -1)
    op("G", lambda: g.iota(T.cF[:], [[1, 256]], W, 0, allow_small_or_imprecise_dtypes=True), [], ["cF"])
    op("V", lambda: v.memset(T.X[:, GB:N0], 127.0), [], ["Xd"])
    op("V", lambda: v.memset(T.A[:, GB:N0], -1), [], ["Ad"])
    op("V", lambda: v.memset(T.NT0[:, 0:1], 1.0), [], ["NTi0"])
    op("V", lambda: v.memset(T.NT1[:, 0:1], 1.0), [], ["NTi1"])
    op("V", lambda: v.memset(T.PW[:], 0.0), [], ["PW"])

    def ci(j): return T.KI[:, j:j + 1]
    def cf(j): return T.KF[:, j:j + 1]
    def kk(j): return "KF%d" % j
    def m16(j): return T.M16[:, j:j + 1]
    ts(ci(0), T.pI[:], 15, None, Op.bitwise_and, None, ["pI"], ["KI0"])
    ts(ci(1), T.pI[:], 4, None, Op.arith_shift_right, None, ["pI"], ["KI1"])
    ts(ci(4), T.pI[:], 1, None, Op.bitwise_and, None, ["pI"], ["KI4"])
    cp(cf(0), T.pI[:], ["pI"], [kk(0)])
    cp(cf(1), ci(0), ["KI0"], [kk(1)])
    cp(cf(2), ci(1), ["KI1"], [kk(2)])
    ts(ci(5), ci(1), 1, None, Op.bitwise_and, None, ["KI1"], ["KI5"])
    ts(T.cmI[:], T.cI[:, 0:128], 15, None, Op.bitwise_and, None, ["cI"], ["cmI"])
    ts(T.cgI[:], T.cI[:, 0:128], 4, None, Op.arith_shift_right, None, ["cI"], ["cgI"])
    P0, PM, PG = cf(0), cf(1), cf(2)
    c128 = T.cI[:, 0:128]
    ts(T.M16[:], T.cI[:, 0:16], PM, None, Op.is_equal, None, ["cI", kk(1)], ["M16"])
    ts(cf(14), PM, 10.5, -1.5 + 2.0 ** -12, Op.is_lt, Op.mult, [kk(1)], [kk(14)])
    ts(T.tF[:], T.cmI[:], 14.5, -1.0, Op.is_lt, Op.mult, ["cmI"], ["tF"])
    ts(T.SAME[:], T.cgI[:], PG, None, Op.is_equal, None, ["cgI", kk(2)], ["SAME"])
    for nm, f in (("B2", 2.0), ("BN", -1.0), ("B1", 1.0), ("BH", 1.0), ("B4", -4096.0)):
        ts(T[nm][:], T.cI[:, 0:8], PG, f, Op.is_equal, Op.mult, ["cI", kk(2)], [nm])
    tt(T.ZM[:], T.tF[:], T.SAME[:], Op.mult, ["tF", "SAME"], ["ZM"])
    ts(T.DC[:], T.cmI[:], 15, None, Op.is_equal, None, ["cmI"], ["DC"])
    lin(cf(6), PM, 1.0, -256.0, [kk(1)], kk(6))
    lin(cf(15), m16(11), 7.5, 1.0, ["M16"], kk(15))
    lin(cf(13), m16(13), -1.0, 0.0, ["M16"], kk(13))
    lin(cf(16), m16(13), 126.5, cf(15), ["M16", kk(15)], kk(16))
    lin(cf(18), cf(16), 1.0, cf(14), [kk(16), kk(14)], kk(18))
    lin(cf(11), m16(15), 1.0, -1.0, ["M16"], kk(11))
    lin(cf(12), m16(14), 1.0, -1.0, ["M16"], kk(12))
    lin(cf(29), m16(12), -11264.0, m16(11), ["M16"], kk(29))
    lin(cf(28), m16(13), 1.0, m16(15), ["M16"], kk(28))
    lin(cf(31), cf(29), 1.0, m16(14), ["M16", kk(29)], kk(31))
    lin(cf(32), cf(28), 512.0, cf(31), [kk(28), kk(31)], kk(32))
    lin(T.M5[:], T.M16[:], 512.0, 0.0, ["M16"], "M5")
    lin(T.MN[:], T.M16[:], 1e6, -1e6, ["M16"], "MN")
    lin(T.AD[:], T.cF[:], m16(14), cf(12), ["cF", "M16", kk(12)], "AD")
    ts(ci(2), ci(0), -1, 30, Op.mult, Op.add, ["KI0"], ["KI2"])
    tt(cf(3), P0, PM, Op.subtract, [kk(0), kk(1)], [kk(3)])
    ts(ci(3), ci(2), 15, None, Op.bitwise_and, None, ["KI2"], ["KI3"])
    ts(cf(4), PM, 14.5, -2048.0, Op.is_lt, Op.mult, [kk(1)], [kk(4)])
    tt(cf(5), ci(3), cf(3), Op.add, ["KI3", kk(3)], [kk(5)])
    ts(T.BLK[:], T.cgI[:], PG, None, Op.is_equal, None, ["cgI", kk(2)], ["BLK"])
    ts(T.PERM[:], c128, cf(5), None, Op.is_equal, None, ["cI", kk(5)], ["PERM"])
    ts(T.MK[:], T.cmI[:], PM, None, Op.is_equal, None, ["cmI", kk(1)], ["MK"])
    ts(cf(7), m16(15), -1000.0, P0, Op.mult, Op.add, ["M16", kk(0)], [kk(7)])
    ts(T.tF[:], c128, cf(7), 1024.0, Op.is_le, Op.mult, ["cI", kk(7)], ["tF"])
    tt(T.TRI[:], T.tF[:], T.SAME[:], Op.mult, ["tF", "SAME"], ["TRI"])
    ts(T.VO[:], T.w0s[:], 8, None, Op.add, None, ["w0s"], ["VO0", "VO1"])
    deferred = []

    def later(f, *a):
        deferred.append(lambda: f(*a))
    later(cp, T.IH[:], T.IB[:], ["IB"], ["IH"])
    later(ts, cf(8), ci(4), 2.0, -1.0, Op.mult, Op.add, ["KI4"], [kk(8)])
    later(ts, cf(9), ci(4), -15.0, 15.0, Op.mult, Op.add, ["KI4"], [kk(9)])
    later(ts, T.TR[:], T.cI[:, 0:16], 16, cf(6), Op.mult, Op.add, ["cI", kk(6)], ["TR"])
    later(ts, cf(19), PM, 10.5, -1.0, Op.is_lt, Op.mult, [kk(1)], [kk(19)])
    for j in range(11):
        later(op, "V", lambda j=j: v.memset(T.PW[:, j::16], 2.0 ** -(j + 1)), ["PW"], ["PWx%d" % j])
    later(tt, T.WB[:], T.PW[:], T.SAME[:], Op.mult, ["PW", "SAME"] + ["PWx%d" % j for j in range(11)], ["WB"])
    later(ts, T.CT[:], T.cI[:], cf(13), cf(18), Op.mult, Op.add, ["cI", kk(13), kk(18)], ["CT"])
    later(ts, T.WH[:], T.IB[:], cf(19), None, Op.mult, None, ["IB", kk(19)], ["WH"])
    later(ts, T.tF[:], T.cmI[:], 11, -1.0, Op.is_equal, Op.mult, ["cmI"], ["tF"])
    later(ts, cf(30), PM, 10.5, 2048.0, Op.is_lt, Op.mult, [kk(1)], [kk(30)])
    later(cp, cf(26), ci(5), ["KI5"], [kk(26)])
    later(ts, cf(27), ci(5), -1.0, 1.0, Op.mult, Op.add, ["KI5"], [kk(27)])
    later(tt, T.WC[:], T.tF[:], T.SAME[:], Op.mult, ["tF", "SAME"], ["WC"])
    for (base, par) in ((20, 27), (23, 26)):
        later(ts, T.KF[:, base:base + 3], T.KF[:, 30:33], cf(par), None, Op.mult, None, [kk(30), kk(31), kk(32), kk(par)], [kk(base)])

    def buf(n, b): return T[n + "%d" % b]
    def key(n, b): return "%s%d" % (n, b)
    def xread(t): return ["X", "Xd"] + (["Xown0", "Xarr0"] if t else [])
    def xwin(t): return T.X[:, GB:N0 + W + K * t]
    def awin(t): return T.A[:, GB:N0 + W + K * t]
    def vo(b): return T.VO[:, 8 * b:8 * b + 8]
    def wb(b): return slice(128 * b, 128 * b + 128)

    def links(t, b):
        op("V", lambda: v.tensor_scalar(buf("AO", b)[:], awin(t).indirect(vo(b)), 8, None, Op.add),
           ["A", "Ad", "Anew0", "Anew1", key("VO", b)], [key("AO", b)])

    def numbers(t, b, hs=(0, 1)):
        for h in hs:
            ac(buf("D", b)[:, 1024 * h:1024 * h + 1024], xwin(t).indirect(buf("AO", b)[:, 64 * h:64 * h + 64]), AF.Copy,
               [key("AO", b)] + xread(t), ["D%d%d" % (b, h)])

    def half(b):
        cp(buf("AH", b)[:], buf("AO", b)[:], [key("AO", b)], [key("AH", b)])

    def gather_y(t, b):
        cp(T.Y[:, wb(b)], xwin(t).indirect(vo(b)), [key("VO", b)] + xread(t), [key("Y", b)])

    def halve(b):
        o = buf("ch", b)[:, 384:512]
        mm(o, T.WR[:, 0:128], buf("Z", b)[:], True, False, ["WR", key("Z", b)], key("ch", b))
        mm(o, T.WR[:, 0:128], T.Y[:, wb(b)], False, True, ["WR", key("Y", b)], key("ch", b))

    def new_z(b):
        ts(buf("Z", b)[:], buf("ch", b)[:, 384:512], MAGIC, MAGIC, Op.add, Op.subtract, [key("ch", b)], [key("Z", b)])

    def spread_z(b):
        for r in range(KZ):
            mm(buf("zp", b)[:, r::KZ], T.IB[:], buf("Z", b)[:], True, True, ["IB", key("Z", b)], key("zp", b))
        mm(buf("dist", b)[:, 0:128], buf("Z", b)[:], T.ZM[:], True, False, ["ZM", key("Z", b)], key("dist", b))

    def bar(b, k):
        for k2 in range(k):
            mm(buf("dist", b)[:, 0:128], buf("SA", b)[:, wb(k2)], T.TRI[:], False, False, ["TRI", key("SA", b)], key("dist", b))

    def sums_d(t, b):
        for i in range(15):
            w = T.B1 if (t == 0 and i == 14) else T.BN
            mm(buf("dist", b)[:, 14 - i:128:16], buf("D", b)[:, i::16], w[:], False, False, ["B1", "BN", "D%d0" % b, "D%d1" % b], key("dist", b))

    PLAN = [[[(0, 4)], [(1, 4)], [(2, 8), (6, 16)], [(3, 8), (7, 16)]], [[(0, 4)], [(1, 4)], [(2, 4)], [(3, 8), (7, 16)]]]

    def max_op(t, b, h, j):
        for (a, st) in PLAN[t][j]:
            r = slice(1024 * h + a, 1024 * h + 1024, st)
            tt(buf("M", b)[:, r], buf("D", b)[:, r], buf("zp", b)[:, 256 * h:256 * h + 256:st // 4], Op.max, ["D%d%d" % (b, h), key("zp", b)], ["M%d%d%d" % (b, h, a)])

    def sums_m(t, b, j):
        for (a, st) in PLAN[t][j]:
            for i in range(a, 16, st):
                mm(buf("dist", b)[:, 14 - i:128:16], buf("M", b)[:, i::16], T.B2[:], False, i == 7,
                   ["B2", "M%d0%d" % (b, a), "M%d1%d" % (b, a)], key("dist", b))

    def sel_a(b):
        ts(buf("NV", b)[:], buf("dist", b)[:, 0:128], 65.5, None, Op.is_ge, None, [key("dist", b)], [key("NV", b)])
        op("V", lambda: v.tensor_tensor_scan(buf("NT", b)[:, 1:129], buf("NV", b)[:], T.DC[:], 1.0, Op.mult, Op.max), [key("NV", b), "DC"], [key("NT", b)])
        o = buf("ch", b)[:, 0:128]
        mm(o, T.PERM[:], buf("AH", b)[:], True, False, ["PERM", key("AH", b)], key("ch", b))
        mm(o, buf("NT", b)[:, 0:128], T.IP[:], False, False, ["IP", key("NTi", b), key("NT", b)], key("ch", b))
        mm(o, buf("NT", b)[:, 1:129], T.IN[:], False, True, ["IN", key("NT", b)], key("ch", b))

    def sel_b(b, k):
        sa = buf("SA", b)[:, wb(k)]
        ts(sa, buf("ch", b)[:, 0:128], cf(4), 0.0, Op.add, Op.max, [key("ch", b), kk(4)], [key("SA", b)])
        mm(buf("ch", b)[:, 128:256], sa, T.BLK[:], True, True, ["BLK", key("SA", b)], key("ch", b))

    def sel_c(b):
        tt(buf("LT", b)[:], buf("ch", b)[:, 128:256], T.MK[:], Op.mult, [key("ch", b), "MK"], [key("LT", b)])
        mm(buf("ch", b)[:, 256:264], buf("LT", b)[:], T.BH[:], True, True, ["BH", key("LT", b)], key("ch", b))

    def sel_d(b):
        cp(vo(b), buf("ch", b)[:, 256:264], [key("ch", b)], [key("VO", b)])

    def bits1(b):
        for lo in (128, 256):
            o = buf("dist", b)[:, lo:lo + 128]
            mm(o, T.IH[:], T.CT[:, wb(b)], True, False, ["IH", "CT"], key("dist", b))
            mm(o, T.WB[:], buf("SA", b)[:, wb(4)], False, lo == 128, ["WB", key("SA", b)], key("dist", b))

    def bits2(b):
        ts(buf("HH", b)[:], buf("dist", b)[:, 128:256], MAGIC, MAGIC, Op.add, Op.subtract, [key("dist", b)], [key("HH", b)])

    def vote(b):
        tt(T.GT[:, wb(b)], T.Y[:, wb(b)], buf("zp", b)[:, 0::KZ], Op.is_gt, [key("Y", b), key("zp", b)], [key("GT", b)])
        o = buf("dist", b)[:, 256:384]
        mm(o, T.WH[:], buf("HH", b)[:], False, False, ["WH", key("HH", b)], key("dist", b))
        mm(o, T.WC[:], T.GT[:, wb(b)], False, True, ["WC", key("GT", b)], key("dist", b))

    def bits3(b):
        ts(T.RB[:, wb(b)], buf("dist", b)[:, 256:384], 0.0, 0.5, Op.is_gt, Op.subtract, [key("dist", b)], [key("RB", b)])

    def left(b, q):
        for (nm, base) in (("LE", 20), ("LO", 23)):
            if q == "V":
                ts(T[nm][:, wb(b)], T.RB[:, wb(b)], cf(base), cf(base + 1 + b), Op.mult, Op.add, [key("RB", b), kk(base)], [key(nm, b)])
            else:
                ac(T[nm][:, wb(b)], T.RB[:, wb(b)], AF.Identity, [key("RB", b), kk(base)], [key(nm, b)], scale=cf(base), bias=cf(base + 1 + b))

    def flipped(b):
        ac(T.FY[:, wb(b)], T.Y[:, wb(b)], AF.Identity, [key("Y", b), kk(8), kk(9)], [key("FY", b)], scale=cf(8), bias=cf(9))

    def turn(b):
        for j in range(4):
            d = (4 * b + j - rank) % 8
            rot = T.WR[:, 128 - 16 * d:256 - 16 * d]
            oo = buf("ch", b)[:, 384 + 32 * j:416 + 32 * j]
            mm(oo, rot, buf("Z", b)[:, 32 * j:32 * j + 32], True, False, ["WR", key("Z", b)], key("ch", b))
            mm(oo, rot, T.Y[:, 128 * b + 32 * j:128 * b + 32 * j + 32], False, True, ["WR", key("Y", b)], key("ch", b))

    sent = [0]

    def send(t, b):
        zs, o = T["ZS%d" % t], buf("ch", b)
        c0 = N0 + W + K * t + 32 * rank
        ts(zs[:, wb(b)], o[:, 384:512], MAGIC, MAGIC, Op.add, Op.subtract, [key("ch", b)], ["ZS%d%d" % (t, b)])
        if rank // 4 == b:
            j = rank % 4
            ts(T.X[:, c0:c0 + 32], o[:, 384 + 32 * j:416 + 32 * j], MAGIC, MAGIC, Op.add, Op.subtract, [key("ch", b)], ["Xown%d" % t])
        deps("G", ["ZS%d%d" % (t, b)], [])
        trs, used = [], set()
        for q in sorted([q for q in range(4 * b, 4 * b + 4) if q != rank], key=lambda q: len(topo.engines(core, T.cores[q]))):
            dst = T.cores[q]
            es = topo.engines(core, dst)
            es = es[0::2] + es[1::2]
            if dst in topo.cores_of(core):
                es = es[::-1]
            e = [x for x in es if x not in used][0]
            used.add(e)
            rid, pid = topo.addr(dst, core)
            trs.append(RemoteDMATransfer(dst_ids=[DstId(rid=rid, pnc=pid)], dma_engine_mask=1 << e, remote_sem=sem["arr%d" % t],
                                         src=zs[:, 32 * q:32 * q + 32], dst=T.X[:, c0:c0 + 32]))
        g.remote_dma_fused(trs, local_sem=sem["snt"])
        sent[0] += len(trs)

    def pairs(bk, lo, gg, c, first, last, kb):
        a, nm = gg // 2, "LE" if gg % 2 == 0 else "LO"
        tri = first <= 128 * c < last
        mm(bk[:, lo:lo + last - first], T[nm][32 * a:32 * a + 32, wb(c)], T.RB[32 * a:32 * a + 32, first:last], True, not tri,
           [key(nm, c), "RB0"] + (["RB1"] if last > 128 else []), kb)
        if tri:
            mm(bk[:, lo + 128 * c - first:lo + 128 * c - first + 128], T.IB[:], T.T2[:], False, True, ["IB", "T2"], kb)

    def reduce_v(src, j, kb):
        op("V", lambda: v.tensor_reduce(T.ACV[:, j:j + 1], src, AxisListType.X, Op.max), [kb], ["ACV%d" % j])

    def reduce_s(src, n, j, kb):
        o = 256 * (j % 4)
        ac(T.junk[:, o:o + n], src, AF.Relu, [kb], ["ACS%d" % j, "junk%d" % (j % 4)], accum_out=T.ACS[:, j:j + 1])

    def place_v(nm, gg, j, an):
        ts(T[nm][:, 16 * gg:16 * gg + 16], T.M5[:], T[an][:, j:j + 1], 0.0, Op.min, Op.max, ["M5", "%s%d" % (an, j)], ["%s%d" % (nm, gg)])

    def place_s(nm, gg, j):
        ac(T[nm][:, 16 * gg:16 * gg + 16], T.MN[:], AF.Relu, ["MN", "ACS%d" % j], ["%s%d" % (nm, gg)], bias=T.ACS[:, j:j + 1])

    def early(gs):
        kbs = ["eA", "eB", "dist0", "zp0"]
        for gg in gs:
            pairs(T[kbs[gg // 2]], 128 * (gg % 2), gg, 0, 0, 128, kbs[gg // 2])
        for gg in gs:
            reduce_s(T[kbs[gg // 2]][:, 128 * (gg % 2):128 * (gg % 2) + 128], 128, gg, kbs[gg // 2])

    def new_links(t, b):
        op("V", lambda: v.tensor_tensor(T.VAL[:, wb(b)], awin(t).indirect(vo(b)), T.AD[:, wb(b)], Op.max), ["A", "Ad", key("VO", b), "AD"], [key("VAL", b)])
        ts(T.A[:, N0 + W + 128 * b:N0 + W + 128 * b + 128], T.VAL[:, wb(b)], m16(15), cf(11), Op.mult, Op.add, [key("VAL", b), "M16", kk(11)], [key("Anew", b)])

    def final_nodes(b):
        mm(buf("ch", b)[:, 128:256], T.BLK[:], buf("SA", b)[:, wb(4)], True, True, ["BLK", key("SA", b)], key("ch", b))
        ts(T.YV[:, wb(b)], buf("ch", b)[:, 128:256], 8.0, None, Op.subtract, None, [key("ch", b)], [key("YV", b)])

    def late(t):
        banks = [("eA", T.eA), ("eB", T.eB), ("dist0", T.dist0), ("dist1", T.dist1)]
        for p in range(4):
            for gg in (2 * p, 2 * p + 1):
                kb, bk = banks[gg % 4]
                pairs(bk, 0, gg, 0, 128, 256, kb)
                pairs(bk, 256, gg, 1, 0, 256, kb)
            if t and p < 2:
                final_nodes(p)
            for gg in (2 * p, 2 * p + 1):
                kb, bk = banks[gg % 4]
                if gg in (1, 3, 4, 6):
                    reduce_s(bk[:, 0:128], 128, 8 + 2 * gg, kb)
                    reduce_s(bk[:, 256:512], 256, 9 + 2 * gg, kb)
                    place_s("LAB", gg, 8 + 2 * gg)
                    place_s("LBB", gg, 9 + 2 * gg)
                else:
                    reduce_v(bk[:, 0:128], 2 * gg, kb)
                    reduce_v(bk[:, 256:512], 2 * gg + 1, kb)
                    place_v("LAB", gg, 2 * gg, "ACV")
                    place_v("LBB", gg, 2 * gg + 1, "ACV")
        ra, rb, rc = [["%s%d" % (nm, gg) for gg in range(8)] for nm in ("LAA", "LAB", "LBB")]
        for (lo, w, wn) in (((256, T.B1, "B1"),) if t == 0 else ()) + ((288, T.B4, "B4"),):
            oa, ob = T.ch0[:, lo:lo + 8], T.ch0[:, lo + 8:lo + 16]
            isx = wn == "B4"
            if isx:
                mm(oa, T.LT0[:], T.BH[:], True, False, ["BH", "LT0"], "ch0")
            mm(oa, T.LAA[:], w[:], not isx, False, [wn] + ra, "ch0")
            mm(oa, T.LAB[:], w[:], False, True, [wn] + rb, "ch0")
            if isx:
                mm(ob, T.LT1[:], T.BH[:], True, False, ["BH", "LT1"], "ch0")
            mm(ob, T.LBB[:], w[:], not isx, True, [wn] + rc, "ch0")
        if t == 0:
            ts(T.FR[:], T.ch0[:, 256:272], 511.5, -4096.0, Op.is_ge, Op.mult, ["ch0"], ["FR"])
        tt(T.FF[:], T.ch0[:, 288:304], T.TR[:], Op.max, ["ch0", "TR"], ["FF"])
        if t == 0:
            tt(T.FR[:], T.FR[:], T.DV[:], Op.add, ["FR", "DV"], ["FR"])
        ts(T.OFX[:], T.FF[:], float(GB), None, Op.add, None, ["FF"], ["OFX"])
        if t == 0:
            tt(T.FR[:], T.FR[:], T.TR[:], Op.max, ["FR", "TR"], ["FR"])
            ts(T.OFA[:], T.FR[:], float(GB), None, Op.add, None, ["FR"], ["OFA"])
            cp(T.A[:, 0:N0 + W].indirect(T.OFA[:]), T.VAL[:], ["OFA", "VAL0", "VAL1", "Ad"], ["A"])

    def flip(t):
        cp(T.X[:, 0:N0 + W + K * t].indirect(T.OFX[:]), T.FY[:], ["OFX", "FY0", "FY1", "Xd"] + (["Xown0", "Xarr0"] if t else []), ["X"])

    for t in range(RO):
        lastw["Xarr%d" % t] = [("arr%d" % t, 7)]
        links(t, 0)
        if t:
            flip(0)
        numbers(t, 0, (1,))
        links(t, 1)
        numbers(t, 1)
        for b in range(2):
            cp(buf("Z", b)[:], xwin(t).indirect(vo(b)), [key("VO", b)] + xread(t), [key("Z", b)])
            spread_z(b)
            if b == 0:
                cp(T.D0[:, 0:1024], xwin(t).indirect(T.AO0[:, 0:64]), ["AO0"] + xread(t), ["D00"])
        half(0)
        half(1)
        for j in range(4):
            max_op(t, 0, 0, j)
        pend = None
        for k in range(S):
            for b in range(2):
                last = (b, k) == (1, S - 1)
                nb = 1 - b

                def fill(*js):
                    for j in js:
                        if not last:
                            max_op(t, nb, 0, j)
                sums_d(t, b)
                if last:
                    bits2(0)
                for j in range(4):
                    max_op(t, b, 1, j)
                    sums_m(t, b, j)
                if pend:
                    gather_y(t, nb)
                    halve(nb)
                    half(nb)
                sel_a(b)
                if pend:
                    new_z(nb)
                    spread_z(nb)
                if last:
                    vote(0)
                for f in deferred[:4]:
                    f()
                del deferred[:4]
                sel_b(b, k)
                if last:
                    turn(0)
                    bits1(1)
                    bits3(0)
                    left(0, "S")
                    flipped(0)
                    if t == 0:
                        new_links(t, 0)
                fill(0)
                sel_c(b)
                if last:
                    send(t, 0)
                    bits2(1)
                    early(range(0, 4))
                fill(1, 2)
                if pend:
                    bar(*pend)
                pend = None
                sel_d(b)
                if k < S - 1:
                    links(t, b)
                    numbers(t, b)
                    pend = (b, k + 1)
                    fill(3)
                elif b == 0:
                    bits1(0)
                    ac(T.Y[:, wb(0)], xwin(t).indirect(vo(0)), AF.Copy, ["VO0"] + xread(t), ["Y0"])
                    fill(3)
                else:
                    gather_y(t, 1)
                    vote(1)
                    bits3(1)
                    left(1, "V")
                    early(range(4, 8))
                    turn(1)
                    flipped(1)
                    if t == 0:
                        ts(T.DV[:], T.VO[:], 1.0, None, Op.mult, None, ["VO0", "VO1"], ["DV"])
                    send(t, 1)
                    if t == 0:
                        new_links(t, 1)
                    for gg in range(8):
                        place_v("LAA", gg, gg, "ACS")
                    late(t)
    flip(RO - 1)
    deps("S", ["X", "Xd", "Xown0", "Xarr0"], [])
    act.dma_start(T.yx[:, 0:W + K], T.X[:, N0:N0 + W + K]).then_inc(sem.out2, 16)
    deps("Y", ["YV0", "YV1"], [])
    g.sync.dma_start(T.yv[:], T.YV[0::16, :]).then_inc(sem.out1, 16)
    deps("Y", ["Xown1", "Xarr1"], [])
    g.sync.dma_start(T.yx[:, W + K:W + 2 * K], T.X[:, N0 + W + K:N0 + W + 2 * K]).then_inc(sem.out3, 16)
    for s, n in (("qV", cnt["V"]), ("qP", cnt["P"]), ("qS", cnt["S"]), ("qG", cnt["G"]), ("snt", sent[0]), ("arr0", 7), ("arr1", 7),
                 ("out1", 16), ("out2", 16), ("out3", 16), ("ldw", 16), ("ldx", 16), ("ldal", 64), ("ldas", 64), ("ldn", 16)):
        g.wait_ge(sem[s], n)
